import numpy as np
import ml_dtypes


def mxq(x, axis, fmt="e4m3"):
    dtype, down = {"e4m3": (ml_dtypes.float8_e4m3fn, 7), "e5m2": (ml_dtypes.float8_e5m2, 14)}[fmt]
    v = np.moveaxis(np.asarray(x, np.float32).astype(ml_dtypes.bfloat16).astype(np.float64), axis, -1)
    blocks = v.reshape(v.shape[:-1] + (-1, 32))
    amax = np.abs(blocks).max(-1, keepdims=True)
    byte = np.maximum(np.where(amax > 0, np.frexp(amax)[1] - 1 + 127, 0) - down, 1)
    scale = np.exp2(byte - 127.0)
    codes = (blocks / scale).astype(np.float32).astype(dtype).astype(np.float64)
    return np.moveaxis((codes * scale).reshape(v.shape), -1, axis)


WIDE = False


def mx_kscale(k, group=512):
    if not WIDE:
        return np.ones(k)
    levels = np.array([10, -10, 5, -5, 0])
    if group != 512:
        return np.exp2(np.random.permutation(np.resize(levels, k // group))).repeat(group)
    if k % 512:
        return np.exp2(np.random.permutation(np.resize(levels, k // 32))).repeat(32)
    a = np.empty((k // 512, 16))
    for p in range(k // 512):
        a[p, :8] = np.random.permutation(np.resize(levels, 8))
        for g in range(8):
            far = levels[np.abs(levels - a[p, g]) >= 10]
            a[p, g + 8] = far[np.random.randint(len(far))]
    return np.exp2(a.ravel()).repeat(32)


def f64(x):
    return np.asarray(x).astype(np.float64)


G, D, K, M, N = 2, 256, 512, 256, 512


def setup_inputs():
    n = np.random.standard_normal
    s = mx_kscale(D, 0)[:, None]
    u = mx_kscale(K)[:, None]
    return {
        "x": (n((G, D, N)) * s).astype(np.float32),
        "w1": (n((G, D, K)) / np.sqrt(D) / s).astype(np.float32),
        "hs": (np.random.uniform(0.5, 2.0, (G, K, 1)) * u).astype(np.float32),
        "w2": (n((G, K, M)) / np.sqrt(K) / u).astype(np.float32),
        "b": (0.5 * n((G, K, 1))).astype(np.float32),
        "r": n((G, M, N)).astype(np.float32),
    }


def reference(x, w1, hs, w2, b, r):
    xq = mxq(f64(x), 1, "e4m3")
    h = mxq(f64(w1), 1, "e4m3").transpose(0, 2, 1) @ xq
    h = h + f64(b)
    h = (h) * f64(hs)
    y = mxq(f64(w2), 1, "e4m3").transpose(0, 2, 1) @ mxq(h, 1, "e4m3")
    y = y + f64(r)
    return y

@@ -1,0 +1,288 @@
+from contextlib import ExitStack
+
+import concourse.mybir as mybir
+
+G, D, K, M, N = 2, 256, 512, 256, 512
+FLOPS = 2 * G * N * (D * K + K * M)
+
+F32 = mybir.dt.float32
+BF16 = mybir.dt.bfloat16
+U32 = mybir.dt.uint32
+U8 = mybir.dt.uint8
+FP8X4 = mybir.dt.float8_e4m3fn_x4
+ALU = mybir.AluOpType
+ACT = mybir.ActivationFunctionType
+
+P = 128
+PACK = 4
+ROWS = D // PACK
+TILE = 128
+BANK = 512
+CHUNKS = [[0,128],[128,384],[384,512]]
+L1_BANKS = 3
+L2_BANKS = 8 - G * L1_BANKS
+
+ORDER = [
+    ("ld_w1", 0,),
+    ("ld_w1", 1,),
+    ("ld_x", 0,),
+    ("ld_bs",),
+    ("ld_x", 1,),
+    ("ld_x", 2,),
+    ("ld_w2", 0,),
+    ("ld_w2", 1,),
+    ("ld_r", 0,),
+    ("ld_r", 1,),
+    ("iw1", "V", 0, 0, 44,),
+    ("iw1", "S", 0, 44, 64,),
+    ("qw1", 0, 0,),
+    ("qw1", 0, 1,),
+    ("qw1", 0, 2,),
+    ("qw1", 0, 3,),
+    ("iw1", "V", 1, 0, 44,),
+    ("iw1", "S", 1, 44, 64,),
+    ("ix", "V", 0, 0, 64,),
+    ("ix", "S", 0, 64, 128,),
+    ("qw1", 1, 0,),
+    ("qw1", 1, 1,),
+    ("qw1", 1, 2,),
+    ("qw1", 1, 3,),
+    ("qx", 0, 128,),
+    ("bhs",),
+    ("mm1", 0, 128, 0, 2, 0,),
+    ("mm1", 0, 128, 2, 4, 1,),
+    ("ix", "V", 1, 128, 320,),
+    ("ix", "S", 1, 320, 384,),
+    ("e1", "S", 0, 0, 0, 128,),
+    ("e1", "S", 0, 1, 0, 128,),
+    ("e1", "S", 1, 0, 0, 128,),
+    ("e1", "S", 1, 1, 0, 128,),
+    ("e1", "S", 0, 2, 0, 128,),
+    ("e1", "S", 0, 3, 0, 128,),
+    ("e1", "S", 1, 2, 0, 128,),
+    ("e1", "S", 1, 3, 0, 128,),
+    ("qx", 128, 384,),
+    ("ix", "V", 2, 384, 512,),
+    ("mm1", 128, 384, 0, 2, 2,),
+    ("mm1", 128, 384, 2, 4, 0,),
+    ("iw2", "V", 0, 0, 128,),
+    ("qx", 384, 512,),
+    ("ih", "V", 0, 0, 128,),
+    ("mm1", 384, 512, 0, 4, 1,),
+    ("e1", "S", 0, 0, 128, 384,),
+    ("e1", "S", 0, 1, 128, 384,),
+    ("e1", "S", 0, 2, 128, 384,),
+    ("e1", "S", 0, 3, 128, 384,),
+    ("iw2", "V", 0, 128, 256,),
+    ("ih", "V", 1, 0, 128,),
+    ("qw2", 0, 0, 256,),
+    ("qh", 0, 0, 128,),
+    ("iw2", "V", 1, 0, 128,),
+    ("qh", 1, 0, 128,),
+    ("iw2", "S", 1, 128, 256,),
+    ("e1", "S", 1, 0, 128, 384,),
+    ("e1", "S", 1, 1, 128, 384,),
+    ("e1", "S", 1, 2, 128, 384,),
+    ("e1", "S", 1, 3, 128, 384,),
+    ("mm2", 0, 0, 128, 0,),
+    ("ih", "V", 0, 128, 384,),
+    ("qw2", 1, 0, 256,),
+    ("mm2", 1, 0, 128, 1,),
+    ("qh", 0, 128, 384,),
+    ("e2", 0, 0, 128,),
+    ("st", 0, 0, 128,),
+    ("e1", "S", 0, 0, 384, 512,),
+    ("e1", "S", 0, 1, 384, 512,),
+    ("e1", "S", 0, 2, 384, 512,),
+    ("e1", "S", 0, 3, 384, 512,),
+    ("ih", "V", 1, 128, 256,),
+    ("ih", "S", 1, 256, 384,),
+    ("mm2", 0, 128, 384, 0,),
+    ("e2", 1, 0, 128,),
+    ("st", 1, 0, 128,),
+    ("e1", "S", 1, 0, 384, 512,),
+    ("e1", "S", 1, 1, 384, 512,),
+    ("e1", "S", 1, 2, 384, 512,),
+    ("e1", "S", 1, 3, 384, 512,),
+    ("qh", 1, 128, 384,),
+    ("ih", "V", 0, 384, 512,),
+    ("mm2", 1, 128, 384, 1,),
+    ("e2", 0, 128, 384,),
+    ("st", 0, 128, 384,),
+    ("ih", "S", 1, 384, 512,),
+    ("qh", 0, 384, 512,),
+    ("mm2", 0, 384, 512, 0,),
+    ("e2", 1, 128, 384,),
+    ("st", 1, 128, 384,),
+    ("qh", 1, 384, 512,),
+    ("mm2", 1, 384, 512, 1,),
+    ("e2", 0, 384, 512,),
+    ("st", 0, 384, 512,),
+    ("e2", 1, 384, 512,),
+    ("st", 1, 384, 512,),
+]
+
+
+def tile_rows_gmlp_bias_res_kernel(tc, x, w1, hs, w2, b, r, out):
+    nc = tc.nc
+    with ExitStack() as ctx:
+        sb = ctx.enter_context(tc.tile_pool(name="sb", bufs=1))
+        ps = ctx.enter_context(tc.psum_pool(name="ps", bufs=1))
+
+        def tile(name, shape, dtype):
+            return sb.tile(shape, dtype, name=name, align_bytes=64)
+
+        w1_raw = [tile("w1_raw%d" % h, [P, PACK, K // 2], F32) for h in range(2)]
+        w1_bf = tile("w1_bf", [P, PACK, TILE, PACK], BF16)
+        w1_codes = tile("w1_codes", [P, K], U32)
+        w1_scales = tile("w1_scales", [P, K], U8)
+        x_raw = [tile("x_raw%d" % c, [P, PACK, n1 - n0], F32) for c, (n0, n1) in enumerate(CHUNKS)]
+        x_bf = tile("x_bf", [P, N, PACK], BF16)
+        x_codes = tile("x_codes", [P, N], U32)
+        x_scales = tile("x_scales", [P, N], U8)
+        w2_raw = [tile("w2_raw%d" % g, [P, PACK, M], F32) for g in range(G)]
+        w2_bf = tile("w2_bf", [P, G, M, PACK], BF16)
+        w2_codes = tile("w2_codes", [P, G, M], U32)
+        w2_scales = tile("w2_scales", [P, G, M], U8)
+        b_sb = tile("b_sb", [P, G, 8], F32)
+        hs_sb = tile("hs_sb", [P, G, 8], F32)
+        bhs_sb = tile("bhs_sb", [P, G, 8], F32)
+        h_rows = [tile("h_rows%d" % g, [P, PACK, N], BF16) for g in range(G)]
+        h_bf = tile("h_bf", [P, G, N, PACK], BF16)
+        h_codes = tile("h_codes", [P, G, N], U32)
+        h_scales = tile("h_scales", [P, G, N], U8)
+        r_sb = [tile("r_sb%d" % g, [P, 2, N], F32) for g in range(G)]
+        y_sb = [tile("y_sb%d" % g, [P, 2, N], F32) for g in range(G)]
+        z_ps = [[ps.tile([P, BANK], F32, name="z%d_%d" % (g, i)) for i in range(L1_BANKS)] for g in range(G)]
+        y_ps = [ps.tile([P, BANK], F32, name="y%d" % i) for i in range(L2_BANKS)]
+
+        x_hbm = x.rearrange("g (p j) n -> (g p) j n", j=PACK)
+        w1_hbm = w1.rearrange("g (p j) k -> (g p) j k", j=PACK)
+        z_place = {}
+        y_place = {}
+
+        def copy(eng, dst, src):
+            if eng == "V":
+                nc.vector.tensor_copy(out=dst, in_=src)
+            elif src.dtype == F32:
+                nc.scalar.activation(out=dst, in_=src, func=ACT.Identity)
+            else:
+                nc.scalar.copy(out=dst, in_=src)
+
+        def interleave(eng, dst, src):
+            copy(eng, dst.rearrange("p (c i) j -> p c j i", i=4), src.rearrange("p j (c i) -> p c j i", i=4))
+
+        def quantize(codes, scales, src):
+            nc.vector.quantize_mx(out=codes.bitcast(FP8X4), scales=scales, in_=src.rearrange("p n j -> p (n j)"))
+
+        def ld_w1(h):
+            nc.sync.dma_start(out=w1_raw[h][:], in_=w1_hbm[:, :, h * 256 : (h + 1) * 256])
+
+        def ld_x(c):
+            n0, n1 = CHUNKS[c]
+            nc.sync.dma_start(out=x_raw[c][:], in_=x_hbm[:, :, n0:n1])
+
+        def ld_bs():
+            nc.sync.dma_start(out=b_sb[:, :, 0:PACK], in_=b.rearrange("g (s r) o -> s g (r o)", r=PACK))
+            nc.sync.dma_start(out=hs_sb[:, :, 0:PACK], in_=hs.rearrange("g (s r) o -> s g (r o)", r=PACK))
+
+        def bhs():
+            nc.gpsimd.tensor_tensor(out=bhs_sb[:, :, 0:PACK], in0=b_sb[:, :, 0:PACK], in1=hs_sb[:, :, 0:PACK], op=ALU.mult)
+
+        def ld_w2(g):
+            nc.sync.dma_start(out=w2_raw[g][:], in_=w2[g].rearrange("(p j) m -> p j m", j=PACK))
+
+        def ld_r(g):
+            nc.sync.dma_start(out=r_sb[g][:], in_=r[g].rearrange("(t p) n -> p t n", p=P))
+
+        def iw1(eng, h, s0, s1):
+            dst = w1_bf[:, :, 64 * h + s0 : 64 * h + s1, :].rearrange("p r s j -> p s r j")
+            src = w1_raw[h][:, :, PACK * s0 : PACK * s1].rearrange("p j (s r) -> p s r j", r=PACK)
+            copy(eng, dst, src)
+
+        def qw1(h, rr):
+            cols = slice(TILE * rr + 64 * h, TILE * rr + 64 * (h + 1))
+            quantize(w1_codes[:, cols], w1_scales[:, cols], w1_bf[:, rr, 64 * h : 64 * (h + 1), :])
+
+        def ix(eng, c, n0, n1):
+            base = CHUNKS[c][0]
+            interleave(eng, x_bf[:, n0:n1, :], x_raw[c][:, :, n0 - base : n1 - base])
+
+        def qx(n0, n1):
+            quantize(x_codes[:, n0:n1], x_scales[:, n0:n1], x_bf[:, n0:n1, :])
+
+        def iw2(eng, g, m0, m1):
+            interleave(eng, w2_bf[:, g, m0:m1, :], w2_raw[g][:, :, m0:m1])
+
+        def qw2(g, m0, m1):
+            quantize(w2_codes[:, g, m0:m1], w2_scales[:, g, m0:m1], w2_bf[:, g, m0:m1, :])
+
+        def mm1(n0, n1, r0, r1, bank):
+            width = n1 - n0
+            for rr in range(r0, r1):
+                for n in range(n0, n1, TILE):
+                    for g in range(G):
+                        rows = slice(ROWS * g, ROWS * (g + 1))
+                        wcols = slice(TILE * rr, TILE * (rr + 1))
+                        off = (rr - r0) * width + n - n0
+                        nc.tensor.matmul_mx(
+                            out=z_ps[g][bank][:, off : off + TILE],
+                            lhsT=w1_codes[rows, wcols].bitcast(FP8X4),
+                            lhsT_scale=w1_scales[rows, wcols],
+                            rhs=x_codes[rows, n : n + TILE].bitcast(FP8X4),
+                            rhs_scale=x_scales[rows, n : n + TILE],
+                            start=True,
+                            stop=True,
+                        )
+                z_place[n0, rr] = (bank, (rr - r0) * width)
+
+        def e1(eng, g, rr, n0, n1):
+            bank, off = z_place[n0, rr]
+            src = z_ps[g][bank][:, off : off + n1 - n0]
+            dst = h_rows[g][:, rr, n0:n1]
+            if eng == "V":
+                nc.vector.tensor_scalar(
+                    out=dst, in0=src, scalar1=b_sb[:, g, rr : rr + 1], scalar2=hs_sb[:, g, rr : rr + 1],
+                    op0=ALU.add, op1=ALU.mult,
+                )
+            else:
+                nc.scalar.activation(
+                    out=dst, in_=src, func=ACT.Identity, bias=bhs_sb[:, g, rr : rr + 1], scale=hs_sb[:, g, rr : rr + 1]
+                )
+
+        def ih(eng, g, n0, n1):
+            interleave(eng, h_bf[:, g, n0:n1, :], h_rows[g][:, :, n0:n1])
+
+        def qh(g, n0, n1):
+            quantize(h_codes[:, g, n0:n1], h_scales[:, g, n0:n1], h_bf[:, g, n0:n1, :])
+
+        def mm2(g, n0, n1, bank):
+            width = n1 - n0
+            for t in range(2):
+                for n in range(n0, n1, TILE):
+                    off = t * width + n - n0
+                    nc.tensor.matmul_mx(
+                        out=y_ps[bank][:, off : off + TILE],
+                        lhsT=w2_codes[:, g, TILE * t : TILE * (t + 1)].bitcast(FP8X4),
+                        lhsT_scale=w2_scales[:, g, TILE * t : TILE * (t + 1)],
+                        rhs=h_codes[:, g, n : n + TILE].bitcast(FP8X4),
+                        rhs_scale=h_scales[:, g, n : n + TILE],
+                        start=True,
+                        stop=True,
+                    )
+            y_place[g, n0] = bank
+
+        def e2(g, n0, n1):
+            src = y_ps[y_place[g, n0]][:, 0 : 2 * (n1 - n0)].rearrange("p (t n) -> p t n", t=2)
+            nc.vector.tensor_tensor(out=y_sb[g][:, :, n0:n1], in0=src, in1=r_sb[g][:, :, n0:n1], op=ALU.add)
+
+        def st(g, n0, n1):
+            nc.sync.dma_start(out=out[g].rearrange("(t p) n -> p t n", p=P)[:, :, n0:n1], in_=y_sb[g][:, :, n0:n1])
+
+        steps = dict(
+            ld_w1=ld_w1, ld_x=ld_x, ld_bs=ld_bs, bhs=bhs, ld_w2=ld_w2, ld_r=ld_r, iw1=iw1, qw1=qw1, ix=ix, qx=qx,
+            iw2=iw2, qw2=qw2, mm1=mm1, e1=e1, ih=ih, qh=qh, mm2=mm2, e2=e2, st=st,
+        )
+        with tc.manual_schedule():
+            for step in ORDER:
+                steps[step[0]](*step[1:])

@@ -18,108 +18,110 @@ PACK = 4
 ROWS = D // PACK
 TILE = 128
 BANK = 512
+X_LOADS = [[0,128],[128,256],[256,384],[384,512]]
 CHUNKS = [[0,128],[128,384],[384,512]]
-L1_BANKS = 3
+L1_BANKS = 2
 L2_BANKS = 8 - G * L1_BANKS
 
 ORDER = [
     ("ld_w1", 0,),
     ("ld_w1", 1,),
     ("ld_x", 0,),
-    ("ld_bs",),
     ("ld_x", 1,),
+    ("ld_bs",),
     ("ld_x", 2,),
     ("ld_w2", 0,),
+    ("ld_x", 3,),
     ("ld_w2", 1,),
-    ("ld_r", 0,),
-    ("ld_r", 1,),
-    ("iw1", "V", 0, 0, 44,),
-    ("iw1", "S", 0, 44, 64,),
+    ("ld_r", 0, 2,),
+    ("ld_r", 2, 4,),
+    ("iw1", "V", 0, 0, 2,),
+    ("iw1", "S", 0, 2, 4,),
     ("qw1", 0, 0,),
     ("qw1", 0, 1,),
     ("qw1", 0, 2,),
     ("qw1", 0, 3,),
-    ("iw1", "V", 1, 0, 44,),
-    ("iw1", "S", 1, 44, 64,),
-    ("ix", "V", 0, 0, 64,),
-    ("ix", "S", 0, 64, 128,),
+    ("iw1", "V", 1, 0, 2,),
+    ("iw1", "S", 1, 2, 4,),
+    ("ix", "V", 0, 0, 80,),
+    ("ix", "S", 0, 80, 128,),
     ("qw1", 1, 0,),
     ("qw1", 1, 1,),
     ("qw1", 1, 2,),
-    ("qw1", 1, 3,),
     ("qx", 0, 128,),
+    ("qw1", 1, 3,),
+    ("ix", "V", 1, 128, 192,),
+    ("ix", "S", 1, 192, 256,),
     ("bhs",),
-    ("mm1", 0, 128, 0, 2, 0,),
-    ("mm1", 0, 128, 2, 4, 1,),
-    ("ix", "V", 1, 128, 320,),
-    ("ix", "S", 1, 320, 384,),
-    ("e1", "S", 0, 0, 0, 128,),
-    ("e1", "S", 0, 1, 0, 128,),
-    ("e1", "S", 1, 0, 0, 128,),
-    ("e1", "S", 1, 1, 0, 128,),
-    ("e1", "S", 0, 2, 0, 128,),
-    ("e1", "S", 0, 3, 0, 128,),
-    ("e1", "S", 1, 2, 0, 128,),
-    ("e1", "S", 1, 3, 0, 128,),
-    ("qx", 128, 384,),
-    ("ix", "V", 2, 384, 512,),
-    ("mm1", 128, 384, 0, 2, 2,),
-    ("mm1", 128, 384, 2, 4, 0,),
+    ("mm1", 0, 0, 2, 0,),
+    ("mm1", 0, 2, 4, 1,),
+    ("qx", 128, 256,),
+    ("ix", "V", 2, 256, 384,),
+    ("e1", "S", 0, 1, 0,),
+    ("e1", "S", 0, 1, 1,),
+    ("e1", "V", 0, 0, 0,),
+    ("e1", "V", 0, 0, 1,),
+    ("qx", 256, 384,),
+    ("e1", "S", 0, 1, 2,),
+    ("e1", "S", 0, 1, 3,),
+    ("e1", "V", 0, 0, 2,),
+    ("e1", "V", 0, 0, 3,),
+    ("mm1", 1, 0, 2, 0,),
+    ("mm1", 1, 2, 4, 1,),
     ("iw2", "V", 0, 0, 128,),
-    ("qx", 384, 512,),
+    ("iw2", "S", 0, 128, 256,),
     ("ih", "V", 0, 0, 128,),
-    ("mm1", 384, 512, 0, 4, 1,),
-    ("e1", "S", 0, 0, 128, 384,),
-    ("e1", "S", 0, 1, 128, 384,),
-    ("e1", "S", 0, 2, 128, 384,),
-    ("e1", "S", 0, 3, 128, 384,),
-    ("iw2", "V", 0, 128, 256,),
-    ("ih", "V", 1, 0, 128,),
-    ("qw2", 0, 0, 256,),
-    ("qh", 0, 0, 128,),
+    ("ix", "V", 3, 384, 512,),
+    ("ih", "S", 0, 128, 256,),
+    ("qw2", 0, 256,),
+    ("e1", "V", 1, 1, 1,),
+    ("qx", 384, 512,),
+    ("e1", "S", 1, 0, 0,),
+    ("e1", "S", 1, 0, 1,),
+    ("e1", "S", 1, 1, 0,),
     ("iw2", "V", 1, 0, 128,),
-    ("qh", 1, 0, 128,),
-    ("iw2", "S", 1, 128, 256,),
-    ("e1", "S", 1, 0, 128, 384,),
-    ("e1", "S", 1, 1, 128, 384,),
-    ("e1", "S", 1, 2, 128, 384,),
-    ("e1", "S", 1, 3, 128, 384,),
-    ("mm2", 0, 0, 128, 0,),
-    ("ih", "V", 0, 128, 384,),
-    ("qw2", 1, 0, 256,),
-    ("mm2", 1, 0, 128, 1,),
-    ("qh", 0, 128, 384,),
-    ("e2", 0, 0, 128,),
-    ("st", 0, 0, 128,),
-    ("e1", "S", 0, 0, 384, 512,),
-    ("e1", "S", 0, 1, 384, 512,),
-    ("e1", "S", 0, 2, 384, 512,),
-    ("e1", "S", 0, 3, 384, 512,),
+    ("e1", "V", 1, 1, 2,),
+    ("e1", "S", 1, 0, 2,),
+    ("e1", "S", 1, 0, 3,),
+    ("e1", "S", 1, 1, 3,),
+    ("mm1", 2, 0, 4, 0,),
+    ("iw2", "V", 1, 128, 256,),
+    ("qh", 0, 0, 256,),
+    ("qw2", 256, 512,),
+    ("mm2", 0, 0, 4, 0,),
+    ("ih", "S", 1, 0, 128,),
     ("ih", "V", 1, 128, 256,),
-    ("ih", "S", 1, 256, 384,),
-    ("mm2", 0, 128, 384, 0,),
-    ("e2", 1, 0, 128,),
-    ("st", 1, 0, 128,),
-    ("e1", "S", 1, 0, 384, 512,),
-    ("e1", "S", 1, 1, 384, 512,),
-    ("e1", "S", 1, 2, 384, 512,),
-    ("e1", "S", 1, 3, 384, 512,),
-    ("qh", 1, 128, 384,),
-    ("ih", "V", 0, 384, 512,),
-    ("mm2", 1, 128, 384, 1,),
-    ("e2", 0, 128, 384,),
-    ("st", 0, 128, 384,),
-    ("ih", "S", 1, 384, 512,),
-    ("qh", 0, 384, 512,),
-    ("mm2", 0, 384, 512, 0,),
-    ("e2", 1, 128, 384,),
-    ("st", 1, 128, 384,),
-    ("qh", 1, 384, 512,),
-    ("mm2", 1, 384, 512, 1,),
-    ("e2", 0, 384, 512,),
-    ("st", 0, 384, 512,),
-    ("e2", 1, 384, 512,),
-    ("st", 1, 384, 512,),
+    ("ih", "V", 1, 384, 512,),
+    ("qh", 1, 0, 256,),
+    ("mm2", 1, 0, 2, 1,),
+    ("ih", "V", 1, 256, 384,),
+    ("e1", "S", 2, 1, 0,),
+    ("e1", "S", 2, 1, 1,),
+    ("e1", "S", 2, 1, 2,),
+    ("e1", "S", 2, 1, 3,),
+    ("e1", "S", 2, 0, 0,),
+    ("e1", "S", 2, 0, 1,),
+    ("e1", "S", 2, 0, 2,),
+    ("e1", "S", 2, 0, 3,),
+    ("e2", 0, 0, 4,),
+    ("st", 0, 1, 0, 4,),
+    ("qh", 1, 256, 512,),
+    ("mm2", 1, 2, 4, 2,),
+    ("ih", "V", 2, 128, 208,),
+    ("ih", "S", 2, 208, 256,),
+    ("ih", "S", 2, 0, 128,),
+    ("e2", 1, 0, 2,),
+    ("st", 1, 2, 0, 2,),
+    ("qh", 2, 128, 256,),
+    ("qh", 2, 0, 128,),
+    ("mm2", 2, 2, 4, 0,),
+    ("mm2", 2, 0, 2, 3,),
+    ("e2", 1, 2, 4,),
+    ("st", 1, 2, 2, 4,),
+    ("e2", 2, 2, 4,),
+    ("st", 2, 3, 2, 4,),
+    ("e2", 2, 0, 2,),
+    ("st", 2, 3, 0, 2,),
 ]
 
 
@@ -132,32 +134,35 @@ def tile_rows_gmlp_bias_res_kernel(tc, x, w1, hs, w2, b, r, out):
         def tile(name, shape, dtype):
             return sb.tile(shape, dtype, name=name, align_bytes=64)
 
+        widths = [n1 - n0 for n0, n1 in CHUNKS]
         w1_raw = [tile("w1_raw%d" % h, [P, PACK, K // 2], F32) for h in range(2)]
-        w1_bf = tile("w1_bf", [P, PACK, TILE, PACK], BF16)
+        w1_bf = [tile("w1_bf%d" % h, [P, PACK, TILE // 2, PACK], BF16) for h in range(2)]
         w1_codes = tile("w1_codes", [P, K], U32)
         w1_scales = tile("w1_scales", [P, K], U8)
-        x_raw = [tile("x_raw%d" % c, [P, PACK, n1 - n0], F32) for c, (n0, n1) in enumerate(CHUNKS)]
+        x_raw = [tile("x_raw%d" % c, [P, PACK, n1 - n0], F32) for c, (n0, n1) in enumerate(X_LOADS)]
         x_bf = tile("x_bf", [P, N, PACK], BF16)
         x_codes = tile("x_codes", [P, N], U32)
         x_scales = tile("x_scales", [P, N], U8)
         w2_raw = [tile("w2_raw%d" % g, [P, PACK, M], F32) for g in range(G)]
-        w2_bf = tile("w2_bf", [P, G, M, PACK], BF16)
-        w2_codes = tile("w2_codes", [P, G, M], U32)
-        w2_scales = tile("w2_scales", [P, G, M], U8)
+        w2_bf = tile("w2_bf", [P, G * M, PACK], BF16)
+        w2_codes = tile("w2_codes", [P, G * M], U32)
+        w2_scales = tile("w2_scales", [P, G * M], U8)
         b_sb = tile("b_sb", [P, G, 8], F32)
         hs_sb = tile("hs_sb", [P, G, 8], F32)
         bhs_sb = tile("bhs_sb", [P, G, 8], F32)
-        h_rows = [tile("h_rows%d" % g, [P, PACK, N], BF16) for g in range(G)]
-        h_bf = tile("h_bf", [P, G, N, PACK], BF16)
-        h_codes = tile("h_codes", [P, G, N], U32)
-        h_scales = tile("h_scales", [P, G, N], U8)
-        r_sb = [tile("r_sb%d" % g, [P, 2, N], F32) for g in range(G)]
-        y_sb = [tile("y_sb%d" % g, [P, 2, N], F32) for g in range(G)]
+        h_rows = [tile("h_rows%d" % c, [P, PACK, G * w], BF16) for c, w in enumerate(widths)]
+        h_bf = [tile("h_bf%d" % c, [P, G * w, PACK], BF16) for c, w in enumerate(widths)]
+        h_codes = [tile("h_codes%d" % c, [P, G * w], U32) for c, w in enumerate(widths)]
+        h_scales = [tile("h_scales%d" % c, [P, G * w], U8) for c, w in enumerate(widths)]
+        r_sb = tile("r_sb", [P, 4, N], F32)
+        y_sb = [tile("y_sb%d" % c, [P, 4, w], F32) for c, w in enumerate(widths)]
         z_ps = [[ps.tile([P, BANK], F32, name="z%d_%d" % (g, i)) for i in range(L1_BANKS)] for g in range(G)]
         y_ps = [ps.tile([P, BANK], F32, name="y%d" % i) for i in range(L2_BANKS)]
 
         x_hbm = x.rearrange("g (p j) n -> (g p) j n", j=PACK)
         w1_hbm = w1.rearrange("g (p j) k -> (g p) j k", j=PACK)
+        r_hbm = r.rearrange("g (t p) n -> p (g t) n", p=P)
+        out_hbm = out.rearrange("g (t p) n -> p (g t) n", p=P)
         z_place = {}
         y_place = {}
 
@@ -179,7 +184,7 @@ def tile_rows_gmlp_bias_res_kernel(tc, x, w1, hs, w2, b, r, out):
             nc.sync.dma_start(out=w1_raw[h][:], in_=w1_hbm[:, :, h * 256 : (h + 1) * 256])
 
         def ld_x(c):
-            n0, n1 = CHUNKS[c]
+            n0, n1 = X_LOADS[c]
             nc.sync.dma_start(out=x_raw[c][:], in_=x_hbm[:, :, n0:n1])
 
         def ld_bs():
@@ -192,32 +197,33 @@ def tile_rows_gmlp_bias_res_kernel(tc, x, w1, hs, w2, b, r, out):
         def ld_w2(g):
             nc.sync.dma_start(out=w2_raw[g][:], in_=w2[g].rearrange("(p j) m -> p j m", j=PACK))
 
-        def ld_r(g):
-            nc.sync.dma_start(out=r_sb[g][:], in_=r[g].rearrange("(t p) n -> p t n", p=P))
+        def ld_r(q0, q1):
+            nc.sync.dma_start(out=r_sb[:, q0:q1, :], in_=r_hbm[:, q0:q1, :])
 
-        def iw1(eng, h, s0, s1):
-            dst = w1_bf[:, :, 64 * h + s0 : 64 * h + s1, :].rearrange("p r s j -> p s r j")
-            src = w1_raw[h][:, :, PACK * s0 : PACK * s1].rearrange("p j (s r) -> p s r j", r=PACK)
+        def iw1(eng, h, r0, r1):
+            dst = w1_bf[h][:, r0:r1, :, :].rearrange("p r s j -> p s r j")
+            src = w1_raw[h][:].rearrange("p j (s r) -> p s r j", r=PACK)[:, :, r0:r1, :]
             copy(eng, dst, src)
 
         def qw1(h, rr):
             cols = slice(TILE * rr + 64 * h, TILE * rr + 64 * (h + 1))
-            quantize(w1_codes[:, cols], w1_scales[:, cols], w1_bf[:, rr, 64 * h : 64 * (h + 1), :])
+            quantize(w1_codes[:, cols], w1_scales[:, cols], w1_bf[h][:, rr, :, :])
 
         def ix(eng, c, n0, n1):
-            base = CHUNKS[c][0]
+            base = X_LOADS[c][0]
             interleave(eng, x_bf[:, n0:n1, :], x_raw[c][:, :, n0 - base : n1 - base])
 
         def qx(n0, n1):
             quantize(x_codes[:, n0:n1], x_scales[:, n0:n1], x_bf[:, n0:n1, :])
 
         def iw2(eng, g, m0, m1):
-            interleave(eng, w2_bf[:, g, m0:m1, :], w2_raw[g][:, :, m0:m1])
+            interleave(eng, w2_bf[:, g * M + m0 : g * M + m1, :], w2_raw[g][:, :, m0:m1])
 
-        def qw2(g, m0, m1):
-            quantize(w2_codes[:, g, m0:m1], w2_scales[:, g, m0:m1], w2_bf[:, g, m0:m1, :])
+        def qw2(m0, m1):
+            quantize(w2_codes[:, m0:m1], w2_scales[:, m0:m1], w2_bf[:, m0:m1, :])
 
-        def mm1(n0, n1, r0, r1, bank):
+        def mm1(c, r0, r1, bank):
+            n0, n1 = CHUNKS[c]
             width = n1 - n0
             for rr in range(r0, r1):
                 for n in range(n0, n1, TILE):
@@ -234,12 +240,13 @@ def tile_rows_gmlp_bias_res_kernel(tc, x, w1, hs, w2, b, r, out):
                             start=True,
                             stop=True,
                         )
-                z_place[n0, rr] = (bank, (rr - r0) * width)
+                z_place[c, rr] = (bank, (rr - r0) * width)
 
-        def e1(eng, g, rr, n0, n1):
-            bank, off = z_place[n0, rr]
-            src = z_ps[g][bank][:, off : off + n1 - n0]
-            dst = h_rows[g][:, rr, n0:n1]
+        def e1(eng, c, g, rr):
+            bank, off = z_place[c, rr]
+            w = widths[c]
+            src = z_ps[g][bank][:, off : off + w]
+            dst = h_rows[c][:, rr, g * w : (g + 1) * w]
             if eng == "V":
                 nc.vector.tensor_scalar(
                     out=dst, in0=src, scalar1=b_sb[:, g, rr : rr + 1], scalar2=hs_sb[:, g, rr : rr + 1],
@@ -250,34 +257,37 @@ def tile_rows_gmlp_bias_res_kernel(tc, x, w1, hs, w2, b, r, out):
                     out=dst, in_=src, func=ACT.Identity, bias=bhs_sb[:, g, rr : rr + 1], scale=hs_sb[:, g, rr : rr + 1]
                 )
 
-        def ih(eng, g, n0, n1):
-            interleave(eng, h_bf[:, g, n0:n1, :], h_rows[g][:, :, n0:n1])
+        def ih(eng, c, a0, a1):
+            interleave(eng, h_bf[c][:, a0:a1, :], h_rows[c][:, :, a0:a1])
 
-        def qh(g, n0, n1):
-            quantize(h_codes[:, g, n0:n1], h_scales[:, g, n0:n1], h_bf[:, g, n0:n1, :])
+        def qh(c, a0, a1):
+            quantize(h_codes[c][:, a0:a1], h_scales[c][:, a0:a1], h_bf[c][:, a0:a1, :])
 
-        def mm2(g, n0, n1, bank):
-            width = n1 - n0
-            for t in range(2):
-                for n in range(n0, n1, TILE):
-                    off = t * width + n - n0
+        def mm2(c, q0, q1, bank):
+            w = widths[c]
+            for q in range(q0, q1):
+                for n in range(0, w, TILE):
+                    off = (q - q0) * w + n
+                    a = (q // 2) * w + n
                     nc.tensor.matmul_mx(
                         out=y_ps[bank][:, off : off + TILE],
-                        lhsT=w2_codes[:, g, TILE * t : TILE * (t + 1)].bitcast(FP8X4),
-                        lhsT_scale=w2_scales[:, g, TILE * t : TILE * (t + 1)],
-                        rhs=h_codes[:, g, n : n + TILE].bitcast(FP8X4),
-                        rhs_scale=h_scales[:, g, n : n + TILE],
+                        lhsT=w2_codes[:, TILE * q : TILE * (q + 1)].bitcast(FP8X4),
+                        lhsT_scale=w2_scales[:, TILE * q : TILE * (q + 1)],
+                        rhs=h_codes[c][:, a : a + TILE].bitcast(FP8X4),
+                        rhs_scale=h_scales[c][:, a : a + TILE],
                         start=True,
                         stop=True,
                     )
-            y_place[g, n0] = bank
+            y_place[c, q0] = bank
 
-        def e2(g, n0, n1):
-            src = y_ps[y_place[g, n0]][:, 0 : 2 * (n1 - n0)].rearrange("p (t n) -> p t n", t=2)
-            nc.vector.tensor_tensor(out=y_sb[g][:, :, n0:n1], in0=src, in1=r_sb[g][:, :, n0:n1], op=ALU.add)
+        def e2(c, q0, q1):
+            n0, n1 = CHUNKS[c]
+            src = y_ps[y_place[c, q0]][:, 0 : (q1 - q0) * (n1 - n0)].rearrange("p (q n) -> p q n", q=q1 - q0)
+            nc.vector.tensor_tensor(out=y_sb[c][:, q0:q1, :], in0=src, in1=r_sb[:, q0:q1, n0:n1], op=ALU.add)
 
-        def st(g, n0, n1):
-            nc.sync.dma_start(out=out[g].rearrange("(t p) n -> p t n", p=P)[:, :, n0:n1], in_=y_sb[g][:, :, n0:n1])
+        def st(c, c_end, q0, q1):
+            n0, n1 = CHUNKS[c]
+            nc.sync.dma_start(out=out_hbm[:, q0:q1, n0:n1], in_=y_sb[c][:, q0:q1, :])
 
         steps = dict(
             ld_w1=ld_w1, ld_x=ld_x, ld_bs=ld_bs, bhs=bhs, ld_w2=ld_w2, ld_r=ld_r, iw1=iw1, qw1=qw1, ix=ix, qx=qx,

@@ -18,109 +18,98 @@ PACK = 4
 ROWS = D // PACK
 TILE = 128
 BANK = 512
-X_LOADS = [[0,128],[128,256],[256,384],[384,512]]
+X_LOADS = [[0,128],[128,384],[384,512]]
 CHUNKS = [[0,128],[128,384],[384,512]]
 L1_BANKS = 2
 L2_BANKS = 8 - G * L1_BANKS
 
 ORDER = [
     ("ld_w1", 0,),
-    ("ld_w1", 1,),
     ("ld_x", 0,),
+    ("iw1", "V", 0, 4, 44, 128,),
     ("ld_x", 1,),
     ("ld_bs",),
-    ("ld_x", 2,),
-    ("ld_w2", 0,),
-    ("ld_x", 3,),
-    ("ld_w2", 1,),
-    ("ld_r", 0, 2,),
-    ("ld_r", 2, 4,),
-    ("iw1", "V", 0, 0, 2,),
-    ("iw1", "S", 0, 2, 4,),
-    ("qw1", 0, 0,),
-    ("qw1", 0, 1,),
-    ("qw1", 0, 2,),
-    ("qw1", 0, 3,),
-    ("iw1", "V", 1, 0, 2,),
-    ("iw1", "S", 1, 2, 4,),
+    ("iw1", "S", 0, 4, 0, 44,),
     ("ix", "V", 0, 0, 80,),
-    ("ix", "S", 0, 80, 128,),
-    ("qw1", 1, 0,),
-    ("qw1", 1, 1,),
-    ("qw1", 1, 2,),
-    ("qx", 0, 128,),
-    ("qw1", 1, 3,),
-    ("ix", "V", 1, 128, 192,),
-    ("ix", "S", 1, 192, 256,),
+    ("qw1", 0, 2, 0, 128,),
     ("bhs",),
+    ("ix", "S", 0, 80, 128,),
+    ("ix", "S", 1, 128, 256,),
+    ("qx", 0, 128,),
     ("mm1", 0, 0, 2, 0,),
+    ("qw1", 2, 4, 0, 128,),
+    ("ld_w2", 0,),
     ("mm1", 0, 2, 4, 1,),
-    ("qx", 128, 256,),
-    ("ix", "V", 2, 256, 384,),
-    ("e1", "S", 0, 1, 0,),
     ("e1", "S", 0, 1, 1,),
+    ("ld_x", 2,),
+    ("ix", "V", 1, 256, 384,),
+    ("qx", 256, 384,),
+    ("e1", "S", 0, 1, 0,),
+    ("e1", "S", 0, 0, 2,),
     ("e1", "V", 0, 0, 0,),
     ("e1", "V", 0, 0, 1,),
-    ("qx", 256, 384,),
-    ("e1", "S", 0, 1, 2,),
-    ("e1", "S", 0, 1, 3,),
-    ("e1", "V", 0, 0, 2,),
-    ("e1", "V", 0, 0, 3,),
+    ("e1", "S", 0, 0, 3,),
+    ("qx", 128, 256,),
     ("mm1", 1, 0, 2, 0,),
+    ("e1", "V", 0, 1, 2,),
+    ("e1", "V", 0, 1, 3,),
+    ("ld_w2", 1,),
     ("mm1", 1, 2, 4, 1,),
-    ("iw2", "V", 0, 0, 128,),
-    ("iw2", "S", 0, 128, 256,),
+    ("iw2", "V", 0, 128, 256,),
+    ("iw2", "S", 0, 0, 128,),
     ("ih", "V", 0, 0, 128,),
-    ("ix", "V", 3, 384, 512,),
-    ("ih", "S", 0, 128, 256,),
-    ("qw2", 0, 256,),
-    ("e1", "V", 1, 1, 1,),
-    ("qx", 384, 512,),
     ("e1", "S", 1, 0, 0,),
+    ("ld_r", 0, 2,),
+    ("ix", "V", 2, 384, 512,),
+    ("e1", "S", 1, 1, 1,),
     ("e1", "S", 1, 0, 1,),
     ("e1", "S", 1, 1, 0,),
+    ("qw2", 0, 256,),
+    ("qx", 384, 512,),
+    ("e1", "V", 1, 0, 3,),
+    ("ld_r", 2, 4,),
+    ("e1", "S", 1, 1, 2,),
+    ("ih", "V", 0, 128, 256,),
     ("iw2", "V", 1, 0, 128,),
-    ("e1", "V", 1, 1, 2,),
     ("e1", "S", 1, 0, 2,),
-    ("e1", "S", 1, 0, 3,),
-    ("e1", "S", 1, 1, 3,),
-    ("mm1", 2, 0, 4, 0,),
     ("iw2", "V", 1, 128, 256,),
     ("qh", 0, 0, 256,),
-    ("qw2", 256, 512,),
-    ("mm2", 0, 0, 4, 0,),
+    ("e1", "S", 1, 1, 3,),
+    ("mm1", 2, 0, 4, 0,),
     ("ih", "S", 1, 0, 128,),
-    ("ih", "V", 1, 128, 256,),
-    ("ih", "V", 1, 384, 512,),
-    ("qh", 1, 0, 256,),
-    ("mm2", 1, 0, 2, 1,),
-    ("ih", "V", 1, 256, 384,),
-    ("e1", "S", 2, 1, 0,),
-    ("e1", "S", 2, 1, 1,),
-    ("e1", "S", 2, 1, 2,),
+    ("ih", "S", 1, 384, 512,),
     ("e1", "S", 2, 1, 3,),
-    ("e1", "S", 2, 0, 0,),
-    ("e1", "S", 2, 0, 1,),
-    ("e1", "S", 2, 0, 2,),
+    ("qw2", 256, 512,),
+    ("e1", "V", 2, 0, 1,),
+    ("e1", "S", 2, 1, 0,),
+    ("ih", "V", 1, 128, 256,),
+    ("e1", "S", 2, 1, 2,),
+    ("e1", "S", 2, 1, 1,),
+    ("mm2", 0, 0, 4, 0,),
+    ("ih", "V", 1, 256, 384,),
+    ("qh", 1, 0, 256,),
+    ("qh", 1, 256, 512,),
+    ("mm2", 1, 0, 2, 1,),
     ("e1", "S", 2, 0, 3,),
     ("e2", 0, 0, 4,),
-    ("st", 0, 1, 0, 4,),
-    ("qh", 1, 256, 512,),
-    ("mm2", 1, 2, 4, 2,),
+    ("e1", "S", 2, 0, 0,),
+    ("e1", "S", 2, 0, 2,),
     ("ih", "V", 2, 128, 208,),
+    ("mm2", 1, 2, 4, 2,),
+    ("e2", 1, 0, 2,),
     ("ih", "S", 2, 208, 256,),
     ("ih", "S", 2, 0, 128,),
-    ("e2", 1, 0, 2,),
-    ("st", 1, 2, 0, 2,),
+    ("st", 0, 1, 0, 4,),
     ("qh", 2, 128, 256,),
+    ("e2", 1, 2, 4,),
     ("qh", 2, 0, 128,),
     ("mm2", 2, 2, 4, 0,),
-    ("mm2", 2, 0, 2, 3,),
-    ("e2", 1, 2, 4,),
-    ("st", 1, 2, 2, 4,),
+    ("st", 1, 2, 0, 2,),
     ("e2", 2, 2, 4,),
-    ("st", 2, 3, 2, 4,),
+    ("st", 1, 2, 2, 4,),
+    ("mm2", 2, 0, 2, 3,),
     ("e2", 2, 0, 2,),
+    ("st", 2, 3, 2, 4,),
     ("st", 2, 3, 0, 2,),
 ]
 
@@ -135,8 +124,8 @@ def tile_rows_gmlp_bias_res_kernel(tc, x, w1, hs, w2, b, r, out):
             return sb.tile(shape, dtype, name=name, align_bytes=64)
 
         widths = [n1 - n0 for n0, n1 in CHUNKS]
-        w1_raw = [tile("w1_raw%d" % h, [P, PACK, K // 2], F32) for h in range(2)]
-        w1_bf = [tile("w1_bf%d" % h, [P, PACK, TILE // 2, PACK], BF16) for h in range(2)]
+        w1_raw = tile("w1_raw", [P, PACK, K], F32)
+        w1_bf = tile("w1_bf", [P, PACK, TILE, PACK], BF16)
         w1_codes = tile("w1_codes", [P, K], U32)
         w1_scales = tile("w1_scales", [P, K], U8)
         x_raw = [tile("x_raw%d" % c, [P, PACK, n1 - n0], F32) for c, (n0, n1) in enumerate(X_LOADS)]
@@ -181,7 +170,7 @@ def tile_rows_gmlp_bias_res_kernel(tc, x, w1, hs, w2, b, r, out):
             nc.vector.quantize_mx(out=codes.bitcast(FP8X4), scales=scales, in_=src.rearrange("p n j -> p (n j)"))
 
         def ld_w1(h):
-            nc.sync.dma_start(out=w1_raw[h][:], in_=w1_hbm[:, :, h * 256 : (h + 1) * 256])
+            nc.sync.dma_start(out=w1_raw[:], in_=w1_hbm)
 
         def ld_x(c):
             n0, n1 = X_LOADS[c]
@@ -200,14 +189,14 @@ def tile_rows_gmlp_bias_res_kernel(tc, x, w1, hs, w2, b, r, out):
         def ld_r(q0, q1):
             nc.sync.dma_start(out=r_sb[:, q0:q1, :], in_=r_hbm[:, q0:q1, :])
 
-        def iw1(eng, h, r0, r1):
-            dst = w1_bf[h][:, r0:r1, :, :].rearrange("p r s j -> p s r j")
-            src = w1_raw[h][:].rearrange("p j (s r) -> p s r j", r=PACK)[:, :, r0:r1, :]
+        def iw1(eng, r0, r1, s0, s1):
+            dst = w1_bf[:, r0:r1, s0:s1, :].rearrange("p r s j -> p s r j")
+            src = w1_raw[:].rearrange("p j (s r) -> p s r j", r=PACK)[:, s0:s1, r0:r1, :]
             copy(eng, dst, src)
 
-        def qw1(h, rr):
-            cols = slice(TILE * rr + 64 * h, TILE * rr + 64 * (h + 1))
-            quantize(w1_codes[:, cols], w1_scales[:, cols], w1_bf[h][:, rr, :, :])
+        def qw1(r0, r1, s0, s1):
+            cols = slice(TILE * r0, TILE * r1)
+            quantize(w1_codes[:, cols], w1_scales[:, cols], w1_bf[:, r0:r1, :, :].rearrange("p r s j -> p (r s) j"))
 
         def ix(eng, c, n0, n1):
             base = X_LOADS[c][0]

@@ -11,107 +11,22 @@ U32 = mybir.dt.uint32
 U8 = mybir.dt.uint8
 FP8X4 = mybir.dt.float8_e4m3fn_x4
 ALU = mybir.AluOpType
-ACT = mybir.ActivationFunctionType
+IDENTITY = mybir.ActivationFunctionType.Identity
 
 P = 128
 PACK = 4
 ROWS = D // PACK
 TILE = 128
 BANK = 512
-X_LOADS = [[0,128],[128,384],[384,512]]
-CHUNKS = [[0,128],[128,384],[384,512]]
-L1_BANKS = 2
-L2_BANKS = 8 - G * L1_BANKS
-
-ORDER = [
-    ("ld_w1", 0,),
-    ("ld_x", 0,),
-    ("iw1", "V", 0, 4, 44, 128,),
-    ("ld_x", 1,),
-    ("ld_bs",),
-    ("iw1", "S", 0, 4, 0, 44,),
-    ("ix", "V", 0, 0, 80,),
-    ("qw1", 0, 2, 0, 128,),
-    ("bhs",),
-    ("ix", "S", 0, 80, 128,),
-    ("ix", "S", 1, 128, 256,),
-    ("qx", 0, 128,),
-    ("mm1", 0, 0, 2, 0,),
-    ("qw1", 2, 4, 0, 128,),
-    ("ld_w2", 0,),
-    ("mm1", 0, 2, 4, 1,),
-    ("e1", "S", 0, 1, 1,),
-    ("ld_x", 2,),
-    ("ix", "V", 1, 256, 384,),
-    ("qx", 256, 384,),
-    ("e1", "S", 0, 1, 0,),
-    ("e1", "S", 0, 0, 2,),
-    ("e1", "V", 0, 0, 0,),
-    ("e1", "V", 0, 0, 1,),
-    ("e1", "S", 0, 0, 3,),
-    ("qx", 128, 256,),
-    ("mm1", 1, 0, 2, 0,),
-    ("e1", "V", 0, 1, 2,),
-    ("e1", "V", 0, 1, 3,),
-    ("ld_w2", 1,),
-    ("mm1", 1, 2, 4, 1,),
-    ("iw2", "V", 0, 128, 256,),
-    ("iw2", "S", 0, 0, 128,),
-    ("ih", "V", 0, 0, 128,),
-    ("e1", "S", 1, 0, 0,),
-    ("ld_r", 0, 2,),
-    ("ix", "V", 2, 384, 512,),
-    ("e1", "S", 1, 1, 1,),
-    ("e1", "S", 1, 0, 1,),
-    ("e1", "S", 1, 1, 0,),
-    ("qw2", 0, 256,),
-    ("qx", 384, 512,),
-    ("e1", "V", 1, 0, 3,),
-    ("ld_r", 2, 4,),
-    ("e1", "S", 1, 1, 2,),
-    ("ih", "V", 0, 128, 256,),
-    ("iw2", "V", 1, 0, 128,),
-    ("e1", "S", 1, 0, 2,),
-    ("iw2", "V", 1, 128, 256,),
-    ("qh", 0, 0, 256,),
-    ("e1", "S", 1, 1, 3,),
-    ("mm1", 2, 0, 4, 0,),
-    ("ih", "S", 1, 0, 128,),
-    ("ih", "S", 1, 384, 512,),
-    ("e1", "S", 2, 1, 3,),
-    ("qw2", 256, 512,),
-    ("e1", "V", 2, 0, 1,),
-    ("e1", "S", 2, 1, 0,),
-    ("ih", "V", 1, 128, 256,),
-    ("e1", "S", 2, 1, 2,),
-    ("e1", "S", 2, 1, 1,),
-    ("mm2", 0, 0, 4, 0,),
-    ("ih", "V", 1, 256, 384,),
-    ("qh", 1, 0, 256,),
-    ("qh", 1, 256, 512,),
-    ("mm2", 1, 0, 2, 1,),
-    ("e1", "S", 2, 0, 3,),
-    ("e2", 0, 0, 4,),
-    ("e1", "S", 2, 0, 0,),
-    ("e1", "S", 2, 0, 2,),
-    ("ih", "V", 2, 128, 208,),
-    ("mm2", 1, 2, 4, 2,),
-    ("e2", 1, 0, 2,),
-    ("ih", "S", 2, 208, 256,),
-    ("ih", "S", 2, 0, 128,),
-    ("st", 0, 1, 0, 4,),
-    ("qh", 2, 128, 256,),
-    ("e2", 1, 2, 4,),
-    ("qh", 2, 0, 128,),
-    ("mm2", 2, 2, 4, 0,),
-    ("st", 1, 2, 0, 2,),
-    ("e2", 2, 2, 4,),
-    ("st", 1, 2, 2, 4,),
-    ("mm2", 2, 0, 2, 3,),
-    ("e2", 2, 0, 2,),
-    ("st", 2, 3, 2, 4,),
-    ("st", 2, 3, 0, 2,),
-]
+Z_BANKS = 2
+Y_BANKS = 4
+GROUP_TILES = M // P
+OUT_TILES = G * GROUP_TILES
+VEC_PAD = 8
+RUN = 4
+CHUNKS = [(0, 128), (128, 384), (384, 512)]
+W1_SCALAR_COLS = 44
+VECTOR_COLS = 80
 
 
 def tile_rows_gmlp_bias_res_kernel(tc, x, w1, hs, w2, b, r, out):
@@ -128,7 +43,7 @@ def tile_rows_gmlp_bias_res_kernel(tc, x, w1, hs, w2, b, r, out):
         w1_bf = tile("w1_bf", [P, PACK, TILE, PACK], BF16)
         w1_codes = tile("w1_codes", [P, K], U32)
         w1_scales = tile("w1_scales", [P, K], U8)
-        x_raw = [tile("x_raw%d" % c, [P, PACK, n1 - n0], F32) for c, (n0, n1) in enumerate(X_LOADS)]
+        x_raw = [tile("x_raw%d" % c, [P, PACK, w], F32) for c, w in enumerate(widths)]
         x_bf = tile("x_bf", [P, N, PACK], BF16)
         x_codes = tile("x_codes", [P, N], U32)
         x_scales = tile("x_scales", [P, N], U8)
@@ -136,17 +51,17 @@ def tile_rows_gmlp_bias_res_kernel(tc, x, w1, hs, w2, b, r, out):
         w2_bf = tile("w2_bf", [P, G * M, PACK], BF16)
         w2_codes = tile("w2_codes", [P, G * M], U32)
         w2_scales = tile("w2_scales", [P, G * M], U8)
-        b_sb = tile("b_sb", [P, G, 8], F32)
-        hs_sb = tile("hs_sb", [P, G, 8], F32)
-        bhs_sb = tile("bhs_sb", [P, G, 8], F32)
-        h_rows = [tile("h_rows%d" % c, [P, PACK, G * w], BF16) for c, w in enumerate(widths)]
+        b_sb = tile("b_sb", [P, G, VEC_PAD], F32)
+        hs_sb = tile("hs_sb", [P, G, VEC_PAD], F32)
+        bhs_sb = tile("bhs_sb", [P, G, VEC_PAD], F32)
+        h_raw = [tile("h_raw%d" % c, [P, PACK, G * w], BF16) for c, w in enumerate(widths)]
         h_bf = [tile("h_bf%d" % c, [P, G * w, PACK], BF16) for c, w in enumerate(widths)]
         h_codes = [tile("h_codes%d" % c, [P, G * w], U32) for c, w in enumerate(widths)]
         h_scales = [tile("h_scales%d" % c, [P, G * w], U8) for c, w in enumerate(widths)]
-        r_sb = tile("r_sb", [P, 4, N], F32)
-        y_sb = [tile("y_sb%d" % c, [P, 4, w], F32) for c, w in enumerate(widths)]
-        z_ps = [[ps.tile([P, BANK], F32, name="z%d_%d" % (g, i)) for i in range(L1_BANKS)] for g in range(G)]
-        y_ps = [ps.tile([P, BANK], F32, name="y%d" % i) for i in range(L2_BANKS)]
+        r_sb = tile("r_sb", [P, OUT_TILES, N], F32)
+        out_sb = [tile("out_sb%d" % c, [P, OUT_TILES, w], F32) for c, w in enumerate(widths)]
+        z_ps = [[ps.tile([P, BANK], F32, name="z%d_%d" % (g, i)) for i in range(Z_BANKS)] for g in range(G)]
+        y_ps = [ps.tile([P, BANK], F32, name="y%d" % i) for i in range(Y_BANKS)]
 
         x_hbm = x.rearrange("g (p j) n -> (g p) j n", j=PACK)
         w1_hbm = w1.rearrange("g (p j) k -> (g p) j k", j=PACK)
@@ -156,72 +71,60 @@ def tile_rows_gmlp_bias_res_kernel(tc, x, w1, hs, w2, b, r, out):
         y_place = {}
 
         def copy(eng, dst, src):
-            if eng == "V":
+            if eng is nc.vector:
                 nc.vector.tensor_copy(out=dst, in_=src)
             elif src.dtype == F32:
-                nc.scalar.activation(out=dst, in_=src, func=ACT.Identity)
+                nc.scalar.activation(out=dst, in_=src, func=IDENTITY)
             else:
                 nc.scalar.copy(out=dst, in_=src)
 
         def interleave(eng, dst, src):
-            copy(eng, dst.rearrange("p (c i) j -> p c j i", i=4), src.rearrange("p j (c i) -> p c j i", i=4))
+            copy(eng, dst.rearrange("p (c i) j -> p c j i", i=RUN), src.rearrange("p j (c i) -> p c j i", i=RUN))
 
         def quantize(codes, scales, src):
             nc.vector.quantize_mx(out=codes.bitcast(FP8X4), scales=scales, in_=src.rearrange("p n j -> p (n j)"))
 
-        def ld_w1(h):
-            nc.sync.dma_start(out=w1_raw[:], in_=w1_hbm)
-
-        def ld_x(c):
-            n0, n1 = X_LOADS[c]
+        def load_x(c):
+            n0, n1 = CHUNKS[c]
             nc.sync.dma_start(out=x_raw[c][:], in_=x_hbm[:, :, n0:n1])
 
-        def ld_bs():
-            nc.sync.dma_start(out=b_sb[:, :, 0:PACK], in_=b.rearrange("g (s r) o -> s g (r o)", r=PACK))
-            nc.sync.dma_start(out=hs_sb[:, :, 0:PACK], in_=hs.rearrange("g (s r) o -> s g (r o)", r=PACK))
-
-        def bhs():
-            nc.gpsimd.tensor_tensor(out=bhs_sb[:, :, 0:PACK], in0=b_sb[:, :, 0:PACK], in1=hs_sb[:, :, 0:PACK], op=ALU.mult)
-
-        def ld_w2(g):
+        def load_w2(g):
             nc.sync.dma_start(out=w2_raw[g][:], in_=w2[g].rearrange("(p j) m -> p j m", j=PACK))
 
-        def ld_r(q0, q1):
-            nc.sync.dma_start(out=r_sb[:, q0:q1, :], in_=r_hbm[:, q0:q1, :])
-
-        def iw1(eng, r0, r1, s0, s1):
-            dst = w1_bf[:, r0:r1, s0:s1, :].rearrange("p r s j -> p s r j")
-            src = w1_raw[:].rearrange("p j (s r) -> p s r j", r=PACK)[:, s0:s1, r0:r1, :]
+        def deal_w1(eng, s0, s1):
+            dst = w1_bf[:, :, s0:s1, :].rearrange("p h s j -> p s h j")
+            src = w1_raw[:].rearrange("p j (s h) -> p s h j", h=PACK)[:, s0:s1, :, :]
             copy(eng, dst, src)
 
-        def qw1(r0, r1, s0, s1):
-            cols = slice(TILE * r0, TILE * r1)
-            quantize(w1_codes[:, cols], w1_scales[:, cols], w1_bf[:, r0:r1, :, :].rearrange("p r s j -> p (r s) j"))
+        def quantize_w1(j0, j1):
+            cols = slice(TILE * j0, TILE * j1)
+            quantize(w1_codes[:, cols], w1_scales[:, cols], w1_bf[:, j0:j1, :, :].rearrange("p h s j -> p (h s) j"))
 
-        def ix(eng, c, n0, n1):
-            base = X_LOADS[c][0]
+        def interleave_x(eng, c, n0, n1):
+            base = CHUNKS[c][0]
             interleave(eng, x_bf[:, n0:n1, :], x_raw[c][:, :, n0 - base : n1 - base])
 
-        def qx(n0, n1):
+        def quantize_x(n0, n1):
             quantize(x_codes[:, n0:n1], x_scales[:, n0:n1], x_bf[:, n0:n1, :])
 
-        def iw2(eng, g, m0, m1):
-            interleave(eng, w2_bf[:, g * M + m0 : g * M + m1, :], w2_raw[g][:, :, m0:m1])
+        def interleave_w2(g):
+            interleave(nc.vector, w2_bf[:, g * M : (g + 1) * M, :], w2_raw[g][:])
 
-        def qw2(m0, m1):
-            quantize(w2_codes[:, m0:m1], w2_scales[:, m0:m1], w2_bf[:, m0:m1, :])
+        def quantize_w2(g):
+            cols = slice(g * M, (g + 1) * M)
+            quantize(w2_codes[:, cols], w2_scales[:, cols], w2_bf[:, cols, :])
 
-        def mm1(c, r0, r1, bank):
+        def first_product(c, j0, j1, bank):
             n0, n1 = CHUNKS[c]
-            width = n1 - n0
-            for rr in range(r0, r1):
+            for j in range(j0, j1):
+                first = (j - j0) * widths[c]
+                wcols = slice(TILE * j, TILE * (j + 1))
                 for n in range(n0, n1, TILE):
                     for g in range(G):
                         rows = slice(ROWS * g, ROWS * (g + 1))
-                        wcols = slice(TILE * rr, TILE * (rr + 1))
-                        off = (rr - r0) * width + n - n0
+                        col = first + n - n0
                         nc.tensor.matmul_mx(
-                            out=z_ps[g][bank][:, off : off + TILE],
+                            out=z_ps[g][bank][:, col : col + TILE],
                             lhsT=w1_codes[rows, wcols].bitcast(FP8X4),
                             lhsT_scale=w1_scales[rows, wcols],
                             rhs=x_codes[rows, n : n + TILE].bitcast(FP8X4),
@@ -229,59 +132,127 @@ def tile_rows_gmlp_bias_res_kernel(tc, x, w1, hs, w2, b, r, out):
                             start=True,
                             stop=True,
                         )
-                z_place[c, rr] = (bank, (rr - r0) * width)
+                z_place[c, j] = (bank, first)
 
-        def e1(eng, c, g, rr):
-            bank, off = z_place[c, rr]
+        def hidden(eng, c, g, places):
             w = widths[c]
-            src = z_ps[g][bank][:, off : off + w]
-            dst = h_rows[c][:, rr, g * w : (g + 1) * w]
-            if eng == "V":
-                nc.vector.tensor_scalar(
-                    out=dst, in0=src, scalar1=b_sb[:, g, rr : rr + 1], scalar2=hs_sb[:, g, rr : rr + 1],
-                    op0=ALU.add, op1=ALU.mult,
-                )
-            else:
-                nc.scalar.activation(
-                    out=dst, in_=src, func=ACT.Identity, bias=bhs_sb[:, g, rr : rr + 1], scale=hs_sb[:, g, rr : rr + 1]
-                )
+            for j in places:
+                bank, first = z_place[c, j]
+                src = z_ps[g][bank][:, first : first + w]
+                dst = h_raw[c][:, j, g * w : (g + 1) * w]
+                scale = hs_sb[:, g, j : j + 1]
+                if eng is nc.vector:
+                    nc.vector.tensor_scalar(
+                        out=dst, in0=src, scalar1=b_sb[:, g, j : j + 1], scalar2=scale, op0=ALU.add, op1=ALU.mult
+                    )
+                else:
+                    nc.scalar.activation(out=dst, in_=src, func=IDENTITY, bias=bhs_sb[:, g, j : j + 1], scale=scale)
 
-        def ih(eng, c, a0, a1):
-            interleave(eng, h_bf[c][:, a0:a1, :], h_rows[c][:, :, a0:a1])
+        def interleave_h(eng, c, a0, a1):
+            interleave(eng, h_bf[c][:, a0:a1, :], h_raw[c][:, :, a0:a1])
 
-        def qh(c, a0, a1):
+        def quantize_h(c, a0, a1):
             quantize(h_codes[c][:, a0:a1], h_scales[c][:, a0:a1], h_bf[c][:, a0:a1, :])
 
-        def mm2(c, q0, q1, bank):
+        def second_product(c, q0, q1, bank):
             w = widths[c]
             for q in range(q0, q1):
+                wcols = slice(TILE * q, TILE * (q + 1))
                 for n in range(0, w, TILE):
-                    off = (q - q0) * w + n
-                    a = (q // 2) * w + n
+                    col = (q - q0) * w + n
+                    hfirst = (q // GROUP_TILES) * w + n
+                    hcols = slice(hfirst, hfirst + TILE)
                     nc.tensor.matmul_mx(
-                        out=y_ps[bank][:, off : off + TILE],
-                        lhsT=w2_codes[:, TILE * q : TILE * (q + 1)].bitcast(FP8X4),
-                        lhsT_scale=w2_scales[:, TILE * q : TILE * (q + 1)],
-                        rhs=h_codes[c][:, a : a + TILE].bitcast(FP8X4),
-                        rhs_scale=h_scales[c][:, a : a + TILE],
+                        out=y_ps[bank][:, col : col + TILE],
+                        lhsT=w2_codes[:, wcols].bitcast(FP8X4),
+                        lhsT_scale=w2_scales[:, wcols],
+                        rhs=h_codes[c][:, hcols].bitcast(FP8X4),
+                        rhs_scale=h_scales[c][:, hcols],
                         start=True,
                         stop=True,
                     )
             y_place[c, q0] = bank
 
-        def e2(c, q0, q1):
+        def finish(c, q0, q1):
             n0, n1 = CHUNKS[c]
-            src = y_ps[y_place[c, q0]][:, 0 : (q1 - q0) * (n1 - n0)].rearrange("p (q n) -> p q n", q=q1 - q0)
-            nc.vector.tensor_tensor(out=y_sb[c][:, q0:q1, :], in0=src, in1=r_sb[:, q0:q1, n0:n1], op=ALU.add)
+            sums = y_ps[y_place[c, q0]][:, 0 : (q1 - q0) * widths[c]].rearrange("p (q n) -> p q n", q=q1 - q0)
+            nc.vector.tensor_tensor(out=out_sb[c][:, q0:q1, :], in0=sums, in1=r_sb[:, q0:q1, n0:n1], op=ALU.add)
+            nc.sync.dma_start(out=out_hbm[:, q0:q1, n0:n1], in_=out_sb[c][:, q0:q1, :])
 
-        def st(c, c_end, q0, q1):
-            n0, n1 = CHUNKS[c]
-            nc.sync.dma_start(out=out_hbm[:, q0:q1, n0:n1], in_=y_sb[c][:, q0:q1, :])
-
-        steps = dict(
-            ld_w1=ld_w1, ld_x=ld_x, ld_bs=ld_bs, bhs=bhs, ld_w2=ld_w2, ld_r=ld_r, iw1=iw1, qw1=qw1, ix=ix, qx=qx,
-            iw2=iw2, qw2=qw2, mm1=mm1, e1=e1, ih=ih, qh=qh, mm2=mm2, e2=e2, st=st,
-        )
+        vec, act = nc.vector, nc.scalar
         with tc.manual_schedule():
-            for step in ORDER:
-                steps[step[0]](*step[1:])
+            nc.sync.dma_start(out=w1_raw[:], in_=w1_hbm)
+            load_x(0)
+            load_x(1)
+            nc.sync.dma_start(out=b_sb[:, :, 0:PACK], in_=b.rearrange("g (s j) o -> s g (j o)", j=PACK))
+            nc.sync.dma_start(out=hs_sb[:, :, 0:PACK], in_=hs.rearrange("g (s j) o -> s g (j o)", j=PACK))
+            load_w2(0)
+            load_x(2)
+            load_w2(1)
+            for g in range(G):
+                tiles = slice(GROUP_TILES * g, GROUP_TILES * (g + 1))
+                nc.sync.dma_start(out=r_sb[:, tiles, :], in_=r_hbm[:, tiles, :])
+
+            deal_w1(vec, W1_SCALAR_COLS, TILE)
+            deal_w1(act, 0, W1_SCALAR_COLS)
+            interleave_x(vec, 0, 0, VECTOR_COLS)
+            interleave_x(act, 0, VECTOR_COLS, 128)
+            quantize_w1(0, 2)
+            quantize_x(0, 128)
+            quantize_w1(2, 4)
+            first_product(0, 0, 2, bank=0)
+            first_product(0, 2, 4, bank=1)
+
+            interleave_x(vec, 1, 256, 384)
+            interleave_x(act, 1, 128, 256)
+            nc.vector.tensor_tensor(
+                out=bhs_sb[:, :, 0:PACK], in0=b_sb[:, :, 0:PACK], in1=hs_sb[:, :, 0:PACK], op=ALU.mult
+            )
+            quantize_x(256, 384)
+            hidden(vec, 0, 0, [0])
+            quantize_x(128, 256)
+            hidden(vec, 0, 0, [1])
+            hidden(act, 0, 1, [2, 0, 1])
+            hidden(vec, 0, 1, [3])
+            hidden(act, 0, 0, [2, 3])
+            first_product(1, 0, 2, bank=0)
+            first_product(1, 2, 4, bank=1)
+
+            interleave_w2(0)
+            interleave_h(vec, 0, 0, 128)
+            interleave_h(act, 0, 128, 256)
+            interleave_x(vec, 2, 384, 512)
+            quantize_w2(0)
+            quantize_x(384, 512)
+            hidden(act, 1, 1, [1])
+            hidden(vec, 1, 1, [0])
+            quantize_h(0, 0, 256)
+            hidden(act, 1, 0, [0, 1, 2, 3])
+            hidden(act, 1, 1, [2, 3])
+            first_product(2, 0, 4, bank=0)
+            interleave_w2(1)
+
+            interleave_h(vec, 1, 0, 128)
+            quantize_w2(1)
+            second_product(0, 0, 4, bank=0)
+            interleave_h(act, 1, 128, 256)
+            interleave_h(vec, 1, 256, 512)
+            quantize_h(1, 0, 256)
+            second_product(1, 0, 2, bank=1)
+            quantize_h(1, 256, 512)
+            second_product(1, 2, 4, bank=2)
+            hidden(act, 2, 1, [0, 1, 2, 3])
+            hidden(act, 2, 0, [0, 1, 2, 3])
+
+            finish(0, 0, 4)
+            interleave_h(vec, 2, 128, 128 + VECTOR_COLS)
+            interleave_h(act, 2, 128 + VECTOR_COLS, 256)
+            interleave_h(act, 2, 0, 128)
+            finish(1, 0, 2)
+            quantize_h(2, 128, 256)
+            second_product(2, 2, 4, bank=0)
+            finish(1, 2, 4)
+            quantize_h(2, 0, 128)
+            second_product(2, 0, 2, bank=3)
+            finish(2, 2, 4)
+            finish(2, 0, 2)

from contextlib import ExitStack

import concourse.mybir as mybir

G, D, K, M, N = 2, 256, 512, 256, 512
FLOPS = 2 * G * N * (D * K + K * M)

F32 = mybir.dt.float32
BF16 = mybir.dt.bfloat16
U32 = mybir.dt.uint32
U8 = mybir.dt.uint8
FP8X4 = mybir.dt.float8_e4m3fn_x4
ALU = mybir.AluOpType
IDENTITY = mybir.ActivationFunctionType.Identity

P = 128
PACK = 4
ROWS = D // PACK
TILE = 128
BANK = 512
Z_BANKS = 2
Y_BANKS = 4
GROUP_TILES = M // P
OUT_TILES = G * GROUP_TILES
VEC_PAD = 8
RUN = 4
CHUNKS = [(0, 128), (128, 384), (384, 512)]
W1_SCALAR_COLS = 44
VECTOR_COLS = 80


def tile_rows_gmlp_bias_res_kernel(tc, x, w1, hs, w2, b, r, out):
    nc = tc.nc
    with ExitStack() as ctx:
        sb = ctx.enter_context(tc.tile_pool(name="sb", bufs=1))
        ps = ctx.enter_context(tc.psum_pool(name="ps", bufs=1))

        def tile(name, shape, dtype):
            return sb.tile(shape, dtype, name=name, align_bytes=64)

        widths = [n1 - n0 for n0, n1 in CHUNKS]
        w1_raw = tile("w1_raw", [P, PACK, K], F32)
        w1_bf = tile("w1_bf", [P, PACK, TILE, PACK], BF16)
        w1_codes = tile("w1_codes", [P, K], U32)
        w1_scales = tile("w1_scales", [P, K], U8)
        x_raw = [tile("x_raw%d" % c, [P, PACK, w], F32) for c, w in enumerate(widths)]
        x_bf = tile("x_bf", [P, N, PACK], BF16)
        x_codes = tile("x_codes", [P, N], U32)
        x_scales = tile("x_scales", [P, N], U8)
        w2_raw = [tile("w2_raw%d" % g, [P, PACK, M], F32) for g in range(G)]
        w2_bf = tile("w2_bf", [P, G * M, PACK], BF16)
        w2_codes = tile("w2_codes", [P, G * M], U32)
        w2_scales = tile("w2_scales", [P, G * M], U8)
        b_sb = tile("b_sb", [P, G, VEC_PAD], F32)
        hs_sb = tile("hs_sb", [P, G, VEC_PAD], F32)
        bhs_sb = tile("bhs_sb", [P, G, VEC_PAD], F32)
        h_raw = [tile("h_raw%d" % c, [P, PACK, G * w], BF16) for c, w in enumerate(widths)]
        h_bf = [tile("h_bf%d" % c, [P, G * w, PACK], BF16) for c, w in enumerate(widths)]
        h_codes = [tile("h_codes%d" % c, [P, G * w], U32) for c, w in enumerate(widths)]
        h_scales = [tile("h_scales%d" % c, [P, G * w], U8) for c, w in enumerate(widths)]
        r_sb = tile("r_sb", [P, OUT_TILES, N], F32)
        out_sb = [tile("out_sb%d" % c, [P, OUT_TILES, w], F32) for c, w in enumerate(widths)]
        z_ps = [[ps.tile([P, BANK], F32, name="z%d_%d" % (g, i)) for i in range(Z_BANKS)] for g in range(G)]
        y_ps = [ps.tile([P, BANK], F32, name="y%d" % i) for i in range(Y_BANKS)]

        x_hbm = x.rearrange("g (p j) n -> (g p) j n", j=PACK)
        w1_hbm = w1.rearrange("g (p j) k -> (g p) j k", j=PACK)
        r_hbm = r.rearrange("g (t p) n -> p (g t) n", p=P)
        out_hbm = out.rearrange("g (t p) n -> p (g t) n", p=P)
        z_place = {}
        y_place = {}

        def copy(eng, dst, src):
            if eng is nc.vector:
                nc.vector.tensor_copy(out=dst, in_=src)
            elif src.dtype == F32:
                nc.scalar.activation(out=dst, in_=src, func=IDENTITY)
            else:
                nc.scalar.copy(out=dst, in_=src)

        def interleave(eng, dst, src):
            copy(eng, dst.rearrange("p (c i) j -> p c j i", i=RUN), src.rearrange("p j (c i) -> p c j i", i=RUN))

        def quantize(codes, scales, src):
            nc.vector.quantize_mx(out=codes.bitcast(FP8X4), scales=scales, in_=src.rearrange("p n j -> p (n j)"))

        def load_x(c):
            n0, n1 = CHUNKS[c]
            nc.sync.dma_start(out=x_raw[c][:], in_=x_hbm[:, :, n0:n1])

        def load_w2(g):
            nc.sync.dma_start(out=w2_raw[g][:], in_=w2[g].rearrange("(p j) m -> p j m", j=PACK))

        def deal_w1(eng, s0, s1):
            dst = w1_bf[:, :, s0:s1, :].rearrange("p h s j -> p s h j")
            src = w1_raw[:].rearrange("p j (s h) -> p s h j", h=PACK)[:, s0:s1, :, :]
            copy(eng, dst, src)

        def quantize_w1(j0, j1):
            cols = slice(TILE * j0, TILE * j1)
            quantize(w1_codes[:, cols], w1_scales[:, cols], w1_bf[:, j0:j1, :, :].rearrange("p h s j -> p (h s) j"))

        def interleave_x(eng, c, n0, n1):
            base = CHUNKS[c][0]
            interleave(eng, x_bf[:, n0:n1, :], x_raw[c][:, :, n0 - base : n1 - base])

        def quantize_x(n0, n1):
            quantize(x_codes[:, n0:n1], x_scales[:, n0:n1], x_bf[:, n0:n1, :])

        def interleave_w2(g):
            interleave(nc.vector, w2_bf[:, g * M : (g + 1) * M, :], w2_raw[g][:])

        def quantize_w2(g):
            cols = slice(g * M, (g + 1) * M)
            quantize(w2_codes[:, cols], w2_scales[:, cols], w2_bf[:, cols, :])

        def first_product(c, j0, j1, bank):
            n0, n1 = CHUNKS[c]
            for j in range(j0, j1):
                first = (j - j0) * widths[c]
                wcols = slice(TILE * j, TILE * (j + 1))
                for n in range(n0, n1, TILE):
                    for g in range(G):
                        rows = slice(ROWS * g, ROWS * (g + 1))
                        col = first + n - n0
                        nc.tensor.matmul_mx(
                            out=z_ps[g][bank][:, col : col + TILE],
                            lhsT=w1_codes[rows, wcols].bitcast(FP8X4),
                            lhsT_scale=w1_scales[rows, wcols],
                            rhs=x_codes[rows, n : n + TILE].bitcast(FP8X4),
                            rhs_scale=x_scales[rows, n : n + TILE],
                            start=True,
                            stop=True,
                        )
                z_place[c, j] = (bank, first)

        def hidden(eng, c, g, places):
            w = widths[c]
            for j in places:
                bank, first = z_place[c, j]
                src = z_ps[g][bank][:, first : first + w]
                dst = h_raw[c][:, j, g * w : (g + 1) * w]
                scale = hs_sb[:, g, j : j + 1]
                if eng is nc.vector:
                    nc.vector.tensor_scalar(
                        out=dst, in0=src, scalar1=b_sb[:, g, j : j + 1], scalar2=scale, op0=ALU.add, op1=ALU.mult
                    )
                else:
                    nc.scalar.activation(out=dst, in_=src, func=IDENTITY, bias=bhs_sb[:, g, j : j + 1], scale=scale)

        def interleave_h(eng, c, a0, a1):
            interleave(eng, h_bf[c][:, a0:a1, :], h_raw[c][:, :, a0:a1])

        def quantize_h(c, a0, a1):
            quantize(h_codes[c][:, a0:a1], h_scales[c][:, a0:a1], h_bf[c][:, a0:a1, :])

        def second_product(c, q0, q1, bank):
            w = widths[c]
            for q in range(q0, q1):
                wcols = slice(TILE * q, TILE * (q + 1))
                for n in range(0, w, TILE):
                    col = (q - q0) * w + n
                    hfirst = (q // GROUP_TILES) * w + n
                    hcols = slice(hfirst, hfirst + TILE)
                    nc.tensor.matmul_mx(
                        out=y_ps[bank][:, col : col + TILE],
                        lhsT=w2_codes[:, wcols].bitcast(FP8X4),
                        lhsT_scale=w2_scales[:, wcols],
                        rhs=h_codes[c][:, hcols].bitcast(FP8X4),
                        rhs_scale=h_scales[c][:, hcols],
                        start=True,
                        stop=True,
                    )
            y_place[c, q0] = bank

        def finish(c, q0, q1):
            n0, n1 = CHUNKS[c]
            sums = y_ps[y_place[c, q0]][:, 0 : (q1 - q0) * widths[c]].rearrange("p (q n) -> p q n", q=q1 - q0)
            nc.vector.tensor_tensor(out=out_sb[c][:, q0:q1, :], in0=sums, in1=r_sb[:, q0:q1, n0:n1], op=ALU.add)
            nc.sync.dma_start(out=out_hbm[:, q0:q1, n0:n1], in_=out_sb[c][:, q0:q1, :])

        vec, act = nc.vector, nc.scalar
        with tc.manual_schedule():
            nc.sync.dma_start(out=w1_raw[:], in_=w1_hbm)
            load_x(0)
            load_x(1)
            nc.sync.dma_start(out=b_sb[:, :, 0:PACK], in_=b.rearrange("g (s j) o -> s g (j o)", j=PACK))
            nc.sync.dma_start(out=hs_sb[:, :, 0:PACK], in_=hs.rearrange("g (s j) o -> s g (j o)", j=PACK))
            load_w2(0)
            load_x(2)
            load_w2(1)
            for g in range(G):
                tiles = slice(GROUP_TILES * g, GROUP_TILES * (g + 1))
                nc.sync.dma_start(out=r_sb[:, tiles, :], in_=r_hbm[:, tiles, :])

            deal_w1(vec, W1_SCALAR_COLS, TILE)
            deal_w1(act, 0, W1_SCALAR_COLS)
            interleave_x(vec, 0, 0, VECTOR_COLS)
            interleave_x(act, 0, VECTOR_COLS, 128)
            quantize_w1(0, 2)
            quantize_x(0, 128)
            quantize_w1(2, 4)
            first_product(0, 0, 2, bank=0)
            first_product(0, 2, 4, bank=1)

            interleave_x(vec, 1, 256, 384)
            interleave_x(act, 1, 128, 256)
            nc.vector.tensor_tensor(
                out=bhs_sb[:, :, 0:PACK], in0=b_sb[:, :, 0:PACK], in1=hs_sb[:, :, 0:PACK], op=ALU.mult
            )
            quantize_x(256, 384)
            hidden(vec, 0, 0, [0])
            quantize_x(128, 256)
            hidden(vec, 0, 0, [1])
            hidden(act, 0, 1, [2, 0, 1])
            hidden(vec, 0, 1, [3])
            hidden(act, 0, 0, [2, 3])
            first_product(1, 0, 2, bank=0)
            first_product(1, 2, 4, bank=1)

            interleave_w2(0)
            interleave_h(vec, 0, 0, 128)
            interleave_h(act, 0, 128, 256)
            interleave_x(vec, 2, 384, 512)
            quantize_w2(0)
            quantize_x(384, 512)
            hidden(act, 1, 1, [1])
            hidden(vec, 1, 1, [0])
            quantize_h(0, 0, 256)
            hidden(act, 1, 0, [0, 1, 2, 3])
            hidden(act, 1, 1, [2, 3])
            first_product(2, 0, 4, bank=0)
            interleave_w2(1)

            interleave_h(vec, 1, 0, 128)
            quantize_w2(1)
            second_product(0, 0, 4, bank=0)
            interleave_h(act, 1, 128, 256)
            interleave_h(vec, 1, 256, 512)
            quantize_h(1, 0, 256)
            second_product(1, 0, 2, bank=1)
            quantize_h(1, 256, 512)
            second_product(1, 2, 4, bank=2)
            hidden(act, 2, 1, [0, 1, 2, 3])
            hidden(act, 2, 0, [0, 1, 2, 3])

            finish(0, 0, 4)
            interleave_h(vec, 2, 128, 128 + VECTOR_COLS)
            interleave_h(act, 2, 128 + VECTOR_COLS, 256)
            interleave_h(act, 2, 0, 128)
            finish(1, 0, 2)
            quantize_h(2, 128, 256)
            second_product(2, 2, 4, bank=0)
            finish(1, 2, 4)
            quantize_h(2, 0, 128)
            second_product(2, 0, 2, bank=3)
            finish(2, 2, 4)
            finish(2, 0, 2)
